import numpy as np
import ml_dtypes


def mxq(x, axis, fmt="e4m3"):
    dtype, down = {"e4m3": (ml_dtypes.float8_e4m3fn, 7), "e5m2": (ml_dtypes.float8_e5m2, 14)}[fmt]
    v = np.moveaxis(np.asarray(x, np.float32).astype(ml_dtypes.bfloat16).astype(np.float64), axis, -1)
    blocks = v.reshape(v.shape[:-1] + (-1, 32))
    amax = np.abs(blocks).max(-1, keepdims=True)
    byte = np.maximum(np.where(amax > 0, np.frexp(amax)[1] - 1 + 127, 0) - down, 1)
    scale = np.exp2(byte - 127.0)
    codes = (blocks / scale).astype(np.float32).astype(dtype).astype(np.float64)
    return np.moveaxis((codes * scale).reshape(v.shape), -1, axis)


WIDE = False


def mx_kscale(k):
    if not WIDE:
        return np.ones(k)
    levels = np.array([10, -10, 5, -5, 0])
    if k % 512:
        return np.exp2(np.random.permutation(np.resize(levels, k // 32))).repeat(32)
    a = np.empty((k // 512, 16))
    for p in range(k // 512):
        a[p, :8] = np.random.permutation(np.resize(levels, 8))
        for g in range(8):
            far = levels[np.abs(levels - a[p, g]) >= 10]
            a[p, g + 8] = far[np.random.randint(len(far))]
    return np.exp2(a.ravel()).repeat(32)


BF16 = ml_dtypes.bfloat16


def bf(x):
    return np.asarray(x, np.float32).astype(BF16)


def f64(x):
    return np.asarray(x).astype(np.float64)


E2M1 = np.array([0.0, 0.5, 1.0, 1.5, 2.0, 3.0, 4.0, 6.0, -0.0, -0.5, -1.0, -1.5, -2.0, -3.0, -4.0, -6.0])


def pack_weight(w, fmt):
    k, n = w.shape
    w = f64(bf(w)).reshape(k // 32, 32, n)
    amax = np.abs(w).max(1)
    if fmt == "e4m3":
        byte = np.frexp(amax)[1] - 1 + 127 - 7
    else:
        mant, ex = np.frexp(amax / 6.0)
        byte = np.where(mant > 0.5, ex, ex - 1) + 127
    byte = np.clip(np.where(amax > 0, byte, 1), 1, 254)
    scaled = (w * np.exp2(127.0 - byte)[:, None, :]).reshape(k, n).astype(np.float32)
    by_word = np.ascontiguousarray(scaled.reshape(k // 512, 128, 4, n).transpose(0, 1, 3, 2))
    if fmt == "e4m3":
        words = by_word.astype(ml_dtypes.float8_e4m3fn).view(np.uint8)
    else:
        c = by_word.astype(ml_dtypes.float4_e2m1fn).view(np.uint8) & 0xF
        words = c[..., 0::2] | (c[..., 1::2] << 4)
    return np.ascontiguousarray(words), np.ascontiguousarray(byte.astype(np.uint8).reshape(k // 512, 16, n))


def unpack_weight(words, scales, fmt):
    g, p, n, _ = words.shape
    if fmt == "e4m3":
        vals = np.ascontiguousarray(words).view(ml_dtypes.float8_e4m3fn).astype(np.float64)
    else:
        nib = np.empty((g, p, n, 4), np.uint8)
        nib[..., 0::2] = words & 0xF
        nib[..., 1::2] = words >> 4
        vals = E2M1[nib]
    vals = vals * np.repeat(np.exp2(scales.astype(np.float64) - 127.0), 8, axis=1)[..., None]
    return vals.transpose(0, 1, 3, 2).reshape(g * 512, n)

E4M3FN = np.array([(-1.0 if i & 128 else 1.0) * ((1.0 + (i & 7) / 8.0) * 2.0 ** (((i >> 3) & 15) - 7) if i & 120 else (i & 7) * 2.0 ** -9) for i in range(256)])


def e4m3fn_bytes(y):
    return np.clip(np.asarray(y, np.float64), -448.0, 448.0).astype(np.float32).astype(ml_dtypes.float8_e4m3fn).view(np.uint8)


def e4m3fn_values(b):
    return E4M3FN[b]


B, LQ, LD, D, H = 128, 64, 128, 512, 1024
T = 3
PAD = 1
POOL = 2
P = (LQ // POOL) * (LD // POOL)


def draw0():
    s, t = mx_kscale(D), mx_kscale(P)
    kn = np.random.standard_normal((T, T))
    q = bf(np.random.standard_normal((B, LQ, D)) * s)
    d = bf(np.random.standard_normal((B, LD, D)) / s)
    kern = bf(0.3 * (kn + 0.5 * np.sign(kn)))
    g = bf(np.random.standard_normal(P) * t)
    w_words, w_scales = pack_weight(np.random.standard_normal((P, H)) / np.sqrt(P) / t[:, None], "e4m3")
    b = bf(np.random.standard_normal(H) * 0.3)
    return {
        "q": q,
        "d": d,
        "kern": kern,
        "g": g,
        "w_words": w_words,
        "w_scales": w_scales,
        "b": b,
    }


def match_grid(q, d):
    qq = mxq(f64(q), 2, "e4m3")
    dq = mxq(f64(d), 2, "e4m3")
    return (qq @ dq.transpose(0, 2, 1)) / np.sqrt(D)


def conv3x3(m, kern):
    rows, cols = m.shape[1], m.shape[2]
    mp = np.pad(m, ((0, 0), (PAD, PAD), (PAD, PAD)))
    c = np.zeros_like(m)
    for u in range(T):
        band = mp[:, u:u + rows, :]
        c = c + kern[u, 0] * band[:, :, 0:cols]
        c = c + kern[u, 1] * band[:, :, 1:1 + cols]
        c = c + kern[u, 2] * band[:, :, 2:2 + cols]
    return c


def maxpool2x2(r):
    n, rows, cols = r.shape
    blocks = r.reshape(n, rows // POOL, POOL, cols // POOL, POOL)
    return np.max(blocks, axis=(2, 4))


def core(q, d, kern, g, w_words, w_scales, b):
    m = match_grid(q, d)
    c = conv3x3(m, f64(kern))
    r = np.maximum(c, 0.0)
    p = maxpool2x2(r)
    f = p.reshape(p.shape[0], p.shape[1] * p.shape[2])
    h = f * f64(g)[None, :]
    y = mxq(h, 1, "e4m3") @ unpack_weight(w_words, w_scales, "e4m3")
    return np.maximum(y + f64(b)[None, :], 0.0)


def setup_inputs():
    drawn = draw0()
    full = np.asarray(drawn['d']).astype(np.float64)
    scale = (np.abs(full).reshape(128, 1, 128, 4, 128).max(axis=(2, 4)) / 448.0).astype(np.float32)
    given = {}
    for key, value in drawn.items():
        if key == 'd':
            given['d_bytes'] = e4m3fn_bytes(full / np.repeat(np.repeat(scale.astype(np.float64), 128, axis=1), 128, axis=2))
            given['d_scale'] = scale
        else:
            given[key] = value
    return given


def reference(q, d_bytes, d_scale, kern, g, w_words, w_scales, b):
    return core(q, e4m3fn_values(d_bytes) * np.repeat(np.repeat(d_scale.astype(np.float64), 128, axis=1), 128, axis=2), kern, g, w_words, w_scales, b)

@@ -1,0 +1,286 @@
+from contextlib import ExitStack
+import math
+
+import concourse.mybir as mybir
+from concourse.masks import make_identity
+
+F32 = mybir.dt.float32
+BF16 = mybir.dt.bfloat16
+U32 = mybir.dt.uint32
+U8 = mybir.dt.uint8
+I32 = mybir.dt.int32
+F8 = mybir.dt.float8_e4m3fn
+F8X4 = mybir.dt.float8_e4m3fn_x4
+ALU = mybir.AluOpType
+COPY = mybir.ActivationFunctionType.Copy
+AX = mybir.AxisListType
+
+B, LQ, LD, D, H = 128, 64, 128, 512, 1024
+FEATS = 2048
+FLOPS = 2 * B * LQ * LD * D + 2 * B * FEATS * H + 18 * B * LQ * LD
+
+HP = 4
+STEPS = B // HP
+CH = 4
+CHUNKS = LQ // CH
+S_WIDEN = 1
+
+
+def tile_matchpyramiddotgridmlphidden_d2p_kernel(tc, q, d_bytes, d_scale, kern, g, w_words, w_scales, b, out):
+    nc = tc.nc
+    with ExitStack() as ctx:
+        const = ctx.enter_context(tc.tile_pool(name="const", bufs=1))
+        big = ctx.enter_context(tc.tile_pool(name="big", bufs=1))
+
+        ident = const.tile([128, 128], F32, name="ident")
+        make_identity(nc, ident[:])
+        scl = const.tile([128, B * 4], F32, name="scl")
+        nc.scalar.dma_start(out=scl[:], in_=d_scale.rearrange("a o q -> (a o q)").partition_broadcast(128))
+        kern_b = const.tile([128, 9], BF16, name="kern_b")
+        perm_l = const.tile([128, 128], F32, name="perm_l")
+        perm_r = const.tile([128, 128], F32, name="perm_r")
+        kcol = const.tile([128, 9], F32, name="kcol")
+        mask = const.tile([128, 2], F32, name="mask")
+        g_b = const.tile([128, FEATS], BF16, name="g_b")
+        b_b = const.tile([128, H], BF16, name="b_b")
+        m = big.tile([128, LQ + 2, B], F32, name="m")
+        w_sb = big.tile([128, 4, H], U32, name="w_sb", align_bytes=64)
+        ws = big.tile([128, H], U8, name="ws", align_bytes=64)
+        nc.gpsimd.memset(ws[:].bitcast(I32), 0)
+        nc.gpsimd.memset(m[:, 0, :], 0.0)
+        nc.gpsimd.memset(m[:, LQ + 1, :], 0.0)
+
+        with ExitStack() as ph1:
+            load = ph1.enter_context(tc.tile_pool(name="load", bufs=6))
+            work = ph1.enter_context(tc.tile_pool(name="work", bufs=3))
+            ps_t = ph1.enter_context(tc.psum_pool(name="ps_t", bufs=2))
+            ps_m = ph1.enter_context(tc.psum_pool(name="ps_m", bufs=2))
+
+            dby = {}
+            qraw = {}
+            wide = {}
+            dgrp = {}
+            qgrp = {}
+            dcod = {}
+            qcod = {}
+            dps = {}
+            qps = {}
+            mps = {}
+
+            def s_widens(h, a):
+                return h % 2 == 1 and a >= HP - S_WIDEN
+
+            def do_load(h):
+                n0 = h * HP
+                t = load.tile([128, HP, D], U8, name="dby", align_bytes=64)
+                nc.sync.dma_start(out=t[:], in_=d_bytes[n0 : n0 + HP].rearrange("a r k -> r a k"))
+                dby[h] = t
+                t2 = load.tile([128, HP // 2, D], BF16, name="qraw", align_bytes=64)
+                nc.sync.dma_start(out=t2[:], in_=q[n0 : n0 + HP].rearrange("(t a) i k -> (a i) t k", a=2))
+                qraw[h] = t2
+
+            def do_widen(h):
+                t = work.tile([128, HP, D], BF16, name="wide", align_bytes=64)
+                for a in range(HP):
+                    n = h * HP + a
+                    for k in range(4):
+                        src = dby[h][:, a, 128 * k : 128 * k + 128].bitcast(F8)
+                        sc = scl[:, 4 * n + k : 4 * n + k + 1]
+                        if s_widens(h, a):
+                            nc.scalar.activation(out=t[:, a, 128 * k : 128 * k + 128], in_=src, func=COPY, scale=sc)
+                        else:
+                            dst = t[:, a, :].rearrange("p (u w e) -> p w u e", u=2, e=2)[:, 32 * k : 32 * k + 32]
+                            nc.vector.tensor_scalar(
+                                out=dst, in0=src.rearrange("p (w u e) -> p w u e", u=2, e=2),
+                                scalar1=sc, scalar2=None, op0=ALU.mult)
+                wide[h] = t
+
+            def do_transpose(h):
+                for x in range(HP // 2):
+                    t = ps_t.tile([128, 2, 2, 128], F32, name="dps%d" % x)
+                    for y in range(2):
+                        a = 2 * x + y
+                        words = wide[h][:, a, :].bitcast(F32)
+                        for u in range(2):
+                            src = words[:, u : 256 : 2] if s_widens(h, a) else words[:, 128 * u : 128 * u + 128]
+                            nc.tensor.transpose(t[:, y, u, :], src, ident[:])
+                    dps[h, x] = t
+                t = ps_t.tile([128, 2, 2, 128], F32, name="qps")
+                for y in range(HP // 2):
+                    words = qraw[h][:, y, :].bitcast(F32)
+                    for u in range(2):
+                        nc.tensor.transpose(t[:, y, u, :], words[:, u : 256 : 2], ident[:])
+                qps[h] = t
+
+            def do_evict(h):
+                t = work.tile([128, HP * 128 * 4], BF16, name="dgrp", align_bytes=64)
+                words = t[:].bitcast(F32)
+                for x in range(HP // 2):
+                    nc.scalar.copy(
+                        out=words[:, 512 * x : 512 * x + 512].rearrange("p (t r u) -> p t r u", t=2, u=2),
+                        in_=dps[h, x][:].rearrange("p t u r -> p t r u"))
+                dgrp[h] = t
+                t2 = work.tile([128, HP * 64 * 4], BF16, name="qgrp", align_bytes=64)
+                nc.scalar.copy(
+                    out=t2[:].bitcast(F32).rearrange("p (t r u) -> p t r u", t=2, u=2),
+                    in_=qps[h][:].rearrange("p t u r -> p t r u"))
+                qgrp[h] = t2
+
+            def do_quant(h):
+                c = work.tile([128, HP * 128], U32, name="dcode", align_bytes=64)
+                s = work.tile([128, HP * 128], U8, name="dscal", align_bytes=64)
+                nc.vector.quantize_mx(out=c[:].bitcast(F8X4), scales=s[:], in_=dgrp[h][:])
+                dcod[h] = (c, s)
+                c = work.tile([128, HP * 64], U32, name="qcode", align_bytes=64)
+                s = work.tile([128, HP * 64], U8, name="qscal", align_bytes=64)
+                nc.vector.quantize_mx(out=c[:].bitcast(F8X4), scales=s[:], in_=qgrp[h][:])
+                qcod[h] = (c, s)
+
+            def do_mx(h):
+                if h % 2 == 0:
+                    t = ps_m.tile([128, 2 * HP, LQ], F32, name="mps")
+                    mps[h // 2] = t
+                t = mps[h // 2]
+                for a in range(HP):
+                    nc.tensor.matmul_mx(
+                        out=t[:, (h % 2) * HP + a, :],
+                        lhsT=dcod[h][0][:, 128 * a : 128 * a + 128].bitcast(F8X4),
+                        lhsT_scale=dcod[h][1][:, 128 * a : 128 * a + 128],
+                        rhs=qcod[h][0][:, 64 * a : 64 * a + 64].bitcast(F8X4),
+                        rhs_scale=qcod[h][1][:, 64 * a : 64 * a + 64],
+                        start=True, stop=True)
+
+            def do_mevict(h):
+                if h % 2 == 1:
+                    n0 = (h - 1) * HP
+                    nc.scalar.copy(
+                        out=m[:, 1 : LQ + 1, n0 : n0 + 2 * HP],
+                        in_=mps[h // 2][:].rearrange("p a i -> p i a"))
+
+            AHEAD = 4
+            with tc.manual_schedule():
+                for h in range(AHEAD):
+                    do_load(h)
+                nc.sync.dma_start(out=kern_b[:], in_=kern.rearrange("a b -> (a b)").partition_broadcast(128))
+                for it in range(-1, STEPS + 4):
+                    if 0 <= it + AHEAD + 1 < STEPS and it + AHEAD + 1 >= AHEAD:
+                        do_load(it + AHEAD + 1)
+                    if it + 1 < STEPS:
+                        do_widen(it + 1)
+                    if 0 <= it < STEPS:
+                        do_transpose(it)
+                        do_evict(it)
+                    if 0 <= it - 1 < STEPS:
+                        do_quant(it - 1)
+                    if 0 <= it - 2 < STEPS:
+                        do_mx(it - 2)
+                    if 0 <= it - 3 < STEPS:
+                        do_mevict(it - 3)
+                    if it == 2:
+                        nc.vector.tensor_scalar(out=mask[:, 0:1], in0=ident[:, 127:128], scalar1=-1.0, scalar2=1.0, op0=ALU.mult, op1=ALU.add)
+                        nc.vector.tensor_scalar(out=mask[:, 1:2], in0=ident[:, 0:1], scalar1=-1.0, scalar2=1.0, op0=ALU.mult, op1=ALU.add)
+                        nc.vector.tensor_scalar(out=kcol[:], in0=kern_b[:], scalar1=1.0 / math.sqrt(D), scalar2=None, op0=ALU.mult)
+                        kc = kcol[:].rearrange("p (u v) -> p u v", v=3)
+                        for v in (0, 2):
+                            mk = mask[:, v // 2 : v // 2 + 1]
+                            nc.vector.tensor_scalar(out=kc[:, :, v], in0=kc[:, :, v], scalar1=mk, scalar2=None, op0=ALU.mult)
+                        nc.vector.tensor_copy(out=perm_l[:, 1:128], in_=ident[:, 0:127])
+                        nc.vector.tensor_copy(out=perm_l[:, 0:1], in_=ident[:, 127:128])
+                        nc.vector.tensor_copy(out=perm_r[:, 0:127], in_=ident[:, 1:128])
+                        nc.vector.tensor_copy(out=perm_r[:, 127:128], in_=ident[:, 0:1])
+                for gg in range(4):
+                    nc.sync.dma_start(out=w_sb[:, gg, :].bitcast(I32), in_=w_words[gg].rearrange("p n t -> p (n t)").bitcast(I32))
+                nc.sync.dma_start(out=g_b[:], in_=g.partition_broadcast(128))
+                nc.sync.dma_start(out=b_b[:], in_=b.partition_broadcast(128))
+                for gg in range(4):
+                    for qd in range(4):
+                        nc.sync.dma_start(
+                            out=ws[32 * qd + 4 * gg : 32 * qd + 4 * gg + 4, :].bitcast(I32),
+                            in_=w_scales[gg, 4 * qd : 4 * qd + 4, :].bitcast(I32))
+
+        prod = ctx.enter_context(tc.tile_pool(name="prod", bufs=3))
+        hid = ctx.enter_context(tc.tile_pool(name="hid", bufs=2))
+        ps_c = ctx.enter_context(tc.psum_pool(name="ps_c", bufs=4))
+        ps_h = ctx.enter_context(tc.psum_pool(name="ps_h", bufs=1))
+        ps_y = ctx.enter_context(tc.psum_pool(name="ps_y", bufs=1))
+        y = [ps_y.tile([128, 512], F32, name="y%d" % x) for x in range(2)]
+        hh = big.tile([128, FEATS], BF16, name="hh", align_bytes=64)
+        perms = (perm_l, ident, perm_r)
+        prods = {}
+        cps = {}
+
+        def rows(c, u):
+            return m[:, CH * c + u : CH * c + u + CH, :].rearrange("p i n -> p (i n)")
+
+        def kc1(u, v):
+            return kcol[:, 3 * u + v : 3 * u + v + 1]
+
+        SUMMED = (0, 2)
+        ON_V = [(2, 0), (2, 1), (2, 2)]
+
+        def do_prod(c):
+            t = {}
+            for u, v in ((1, 0), (1, 2), (1, 1), (0, 1)):
+                x = prod.tile([128, CH * B], F32, name="pr%d%d" % (u, v))
+                nc.scalar.activation(out=x[:], in_=rows(c, u), func=COPY, scale=kc1(u, v))
+                t[u, v] = x
+            for u, v in ON_V:
+                x = prod.tile([128, CH * B], F32, name="pr%d%d" % (u, v))
+                nc.vector.tensor_scalar(out=x[:], in0=rows(c, u), scalar1=kc1(u, v), scalar2=None, op0=ALU.mult)
+                t[u, v] = x
+            for v in SUMMED:
+                x = prod.tile([128, CH * B], F32, name="sum%d" % v)
+                nc.vector.scalar_tensor_tensor(out=x[:], in0=rows(c, 0), scalar=kc1(0, v), in1=t[1, v][:], op0=ALU.mult, op1=ALU.add)
+                t[1, v] = x
+            prods[c] = t
+
+        def do_conv(c):
+            ps = ps_c.tile([128, CH, LD], F32, name="cps")
+            t = prods[c]
+            keys = [(2, 0), (2, 1), (2, 2), (0, 1), (1, 1), (1, 0), (1, 2)]
+            for i in range(CH):
+                for n, (u, v) in enumerate(keys):
+                    nc.tensor.matmul(ps[:, i, :], t[u, v][:, B * i : B * i + B], perms[v][:],
+                                     start=(n == 0), stop=(n == len(keys) - 1), is_transpose=True)
+            cps[c] = ps
+
+        def do_pool(c):
+            r = hid.tile([128, CH // 2, LD // 2], F32, name="pooled")
+            nc.vector.tensor_reduce(out=r[:], in_=cps[c][:].rearrange("p (a i) (b j) -> p a b i j", i=2, j=2), axis=AX.XY, op=ALU.max)
+            n = CH // 2 * LD // 2
+            nc.vector.scalar_tensor_tensor(out=hh[:, n * c : n * c + n], in0=r[:].rearrange("p a b -> p (a b)"), scalar=0.0,
+                                           in1=g_b[:, n * c : n * c + n], op0=ALU.max, op1=ALU.mult)
+
+        def do_hidden(gg):
+            hw = hh[:].bitcast(F32)
+            t = ps_h.tile([128, 2, 128], F32, name="hps")
+            for u in range(2):
+                nc.tensor.transpose(t[:, u, :], hw[:, 256 * gg + u : 256 * gg + 256 : 2], ident[:])
+            hg = hid.tile([128, 512], BF16, name="hg", align_bytes=64)
+            nc.scalar.copy(out=hg[:].bitcast(F32).rearrange("p (r u) -> p r u", u=2), in_=t[:].rearrange("p u r -> p r u"))
+            c = hid.tile([128, 128], U32, name="hcode", align_bytes=64)
+            s = hid.tile([128, 128], U8, name="hscal", align_bytes=64)
+            nc.vector.quantize_mx(out=c[:].bitcast(F8X4), scales=s[:], in_=hg[:])
+            for x in range(2):
+                nc.tensor.matmul_mx(
+                    out=y[x][:], lhsT=c[:].bitcast(F8X4), lhsT_scale=s[:],
+                    rhs=w_sb[:, gg, 512 * x : 512 * x + 512].bitcast(F8X4), rhs_scale=ws[4 * gg : 128, 512 * x : 512 * x + 512],
+                    start=(gg == 0), stop=(gg == 3))
+
+        per = CHUNKS // 4
+        with tc.manual_schedule():
+            for it in range(CHUNKS + 3):
+                if it < CHUNKS:
+                    do_prod(it)
+                if 0 <= it - 1 < CHUNKS:
+                    do_conv(it - 1)
+                if 0 <= it - 2 < CHUNKS:
+                    do_pool(it - 2)
+                    if (it - 2) % per == per - 1:
+                        do_hidden((it - 2) // per)
+            for x in range(2):
+                t = hid.tile([128, 512], F32, name="ysum")
+                nc.vector.tensor_tensor(out=t[:], in0=y[x][:], in1=b_b[:, 512 * x : 512 * x + 512], op=ALU.add)
+                o = hid.tile([128, 512], F32, name="yout")
+                nc.scalar.activation(out=o[:], in_=t[:], func=mybir.ActivationFunctionType.Relu)
+                nc.sync.dma_start(out=out[:, 512 * x : 512 * x + 512], in_=o[:])

@@ -13,6 +13,7 @@ F8 = mybir.dt.float8_e4m3fn
 F8X4 = mybir.dt.float8_e4m3fn_x4
 ALU = mybir.AluOpType
 COPY = mybir.ActivationFunctionType.Copy
+RELU = mybir.ActivationFunctionType.Relu
 AX = mybir.AxisListType
 
 B, LQ, LD, D, H = 128, 64, 128, 512, 1024
@@ -21,266 +22,350 @@ FLOPS = 2 * B * LQ * LD * D + 2 * B * FEATS * H + 18 * B * LQ * LD
 
 HP = 4
 STEPS = B // HP
+NQ = 4
+GP = B // NQ
+SPG = STEPS // NQ
+RI = LQ // NQ
 CH = 4
-CHUNKS = LQ // CH
-S_WIDEN = 1
+CPG = RI // CH
+CHUNKS = NQ * CPG
+AHEAD = 5
+BAND = 2
+MAIN = ((("S", 2, 0), ("S", 2, 1), ("V", 0, 1), ("V", 1, 0)), (("S", 2, 2), ("A", 0, 2), ("+", 0, 0), ("V", 1, 1), ("V", 1, 2)))
+LAST = ((("S", 2, 0), ("S", 2, 2), ("V", 1, 0), ("V", 1, 1)), (("S", 2, 1), ("A", 0, 1), ("V", 1, 2), ("+", 0, 0), ("+", 0, 2)))
 
 
 def tile_matchpyramiddotgridmlphidden_d2p_kernel(tc, q, d_bytes, d_scale, kern, g, w_words, w_scales, b, out):
     nc = tc.nc
     with ExitStack() as ctx:
         const = ctx.enter_context(tc.tile_pool(name="const", bufs=1))
-        big = ctx.enter_context(tc.tile_pool(name="big", bufs=1))
+        load = ctx.enter_context(tc.tile_pool(name="load", bufs=6))
+        work = ctx.enter_context(tc.tile_pool(name="work", bufs=3))
+        grid = ctx.enter_context(tc.tile_pool(name="grid", bufs=3))
+        prod = ctx.enter_context(tc.tile_pool(name="prod", bufs=2))
+        hid = ctx.enter_context(tc.tile_pool(name="hid", bufs=2))
+        ps_t = ctx.enter_context(tc.psum_pool(name="ps_t", bufs=4))
+        ps_m = ctx.enter_context(tc.psum_pool(name="ps_m", bufs=1))
+        ps_c = ctx.enter_context(tc.psum_pool(name="ps_c", bufs=2))
+        ps_h = ctx.enter_context(tc.psum_pool(name="ps_h", bufs=1))
 
         ident = const.tile([128, 128], F32, name="ident")
         make_identity(nc, ident[:])
         scl = const.tile([128, B * 4], F32, name="scl")
         nc.scalar.dma_start(out=scl[:], in_=d_scale.rearrange("a o q -> (a o q)").partition_broadcast(128))
+        ones = const.tile([128, 1], F32, name="ones")
+        nc.vector.memset(ones[:], 1.0)
+        scp = const.tile([128, B], F32, name="scp")
+        for x in range(4):
+            nc.gpsimd.tensor_copy(out=scp[32 * x : 32 * x + 32, :], in_=scl[32 * x : 32 * x + 32, :].rearrange("p (n x) -> p n x", x=4)[:, :, x])
         kern_b = const.tile([128, 9], BF16, name="kern_b")
         perm_l = const.tile([128, 128], F32, name="perm_l")
         perm_r = const.tile([128, 128], F32, name="perm_r")
         kcol = const.tile([128, 9], F32, name="kcol")
+        band = const.tile([128, 128], F32, name="band")
         mask = const.tile([128, 2], F32, name="mask")
-        g_b = const.tile([128, FEATS], BF16, name="g_b")
+        g_b = const.tile([128, FEATS // NQ], BF16, name="g_b")
         b_b = const.tile([128, H], BF16, name="b_b")
-        m = big.tile([128, LQ + 2, B], F32, name="m")
-        w_sb = big.tile([128, 4, H], U32, name="w_sb", align_bytes=64)
-        ws = big.tile([128, H], U8, name="ws", align_bytes=64)
+        w_sb = const.tile([128, 4, H], U32, name="w_sb", align_bytes=64)
+        ws = const.tile([128, H], U8, name="ws", align_bytes=64)
+        hg = const.tile([128, 4 * B * 4], BF16, name="hg", align_bytes=64)
         nc.gpsimd.memset(ws[:].bitcast(I32), 0)
-        nc.gpsimd.memset(m[:, 0, :], 0.0)
-        nc.gpsimd.memset(m[:, LQ + 1, :], 0.0)
 
-        with ExitStack() as ph1:
-            load = ph1.enter_context(tc.tile_pool(name="load", bufs=6))
-            work = ph1.enter_context(tc.tile_pool(name="work", bufs=3))
-            ps_t = ph1.enter_context(tc.psum_pool(name="ps_t", bufs=2))
-            ps_m = ph1.enter_context(tc.psum_pool(name="ps_m", bufs=2))
+        dby, qraw, wide, dgrp, qgrp, dcod, qcod, tps, mps, m, prods, cps, pooled, hh = ({} for n in range(14))
+        perms = (perm_l, ident, perm_r)
 
-            dby = {}
-            qraw = {}
-            wide = {}
-            dgrp = {}
-            qgrp = {}
-            dcod = {}
-            qcod = {}
-            dps = {}
-            qps = {}
-            mps = {}
+        def s_widens(h, a):
+            return a >= 2
 
-            def s_widens(h, a):
-                return h % 2 == 1 and a >= HP - S_WIDEN
+        def parts(h):
+            return [(a, 1) for a in range(HP)] if h == 0 else [(0, HP)]
 
-            def do_load(h):
-                n0 = h * HP
-                t = load.tile([128, HP, D], U8, name="dby", align_bytes=64)
-                nc.sync.dma_start(out=t[:], in_=d_bytes[n0 : n0 + HP].rearrange("a r k -> r a k"))
-                dby[h] = t
-                t2 = load.tile([128, HP // 2, D], BF16, name="qraw", align_bytes=64)
-                nc.sync.dma_start(out=t2[:], in_=q[n0 : n0 + HP].rearrange("(t a) i k -> (a i) t k", a=2))
-                qraw[h] = t2
+        def do_load(h):
+            n0 = h * HP
+            t = load.tile([128, HP, D], U8, name="dby", align_bytes=64)
+            for a, n in parts(h):
+                nc.sync.dma_start(out=t[:, a : a + n, :], in_=d_bytes[n0 + a : n0 + a + n].rearrange("a r k -> r a k"))
+            dby[h] = t
+            t2 = load.tile([128, HP // 2, D], BF16, name="qraw", align_bytes=64)
+            nc.sync.dma_start(out=t2[:], in_=q[n0 : n0 + HP].rearrange("(t a) i k -> (a i) t k", a=2))
+            qraw[h] = t2
 
-            def do_widen(h):
-                t = work.tile([128, HP, D], BF16, name="wide", align_bytes=64)
-                for a in range(HP):
-                    n = h * HP + a
-                    for k in range(4):
-                        src = dby[h][:, a, 128 * k : 128 * k + 128].bitcast(F8)
-                        sc = scl[:, 4 * n + k : 4 * n + k + 1]
-                        if s_widens(h, a):
-                            nc.scalar.activation(out=t[:, a, 128 * k : 128 * k + 128], in_=src, func=COPY, scale=sc)
-                        else:
-                            dst = t[:, a, :].rearrange("p (u w e) -> p w u e", u=2, e=2)[:, 32 * k : 32 * k + 32]
-                            nc.vector.tensor_scalar(
-                                out=dst, in0=src.rearrange("p (w u e) -> p w u e", u=2, e=2),
-                                scalar1=sc, scalar2=None, op0=ALU.mult)
-                wide[h] = t
+        def do_widen(h, on_s):
+            if on_s:
+                return
+            t = work.tile([128, 2, HP * 128, 2], BF16, name="wide", align_bytes=64)
+            for a, n in parts(h):
+                nc.vector.tensor_scalar(
+                    out=t[:, :, 128 * a : 128 * (a + n), :].rearrange("p u w e -> p w u e"),
+                    in0=dby[h][:, a : a + n, :].rearrange("p a k -> p (a k)").bitcast(F8).rearrange("p (w u e) -> p w u e", u=2, e=2),
+                    scalar1=ones[:], scalar2=None, op0=ALU.mult)
+            wide[h] = t
 
-            def do_transpose(h):
-                for x in range(HP // 2):
-                    t = ps_t.tile([128, 2, 2, 128], F32, name="dps%d" % x)
-                    for y in range(2):
-                        a = 2 * x + y
-                        words = wide[h][:, a, :].bitcast(F32)
-                        for u in range(2):
-                            src = words[:, u : 256 : 2] if s_widens(h, a) else words[:, 128 * u : 128 * u + 128]
-                            nc.tensor.transpose(t[:, y, u, :], src, ident[:])
-                    dps[h, x] = t
-                t = ps_t.tile([128, 2, 2, 128], F32, name="qps")
-                for y in range(HP // 2):
-                    words = qraw[h][:, y, :].bitcast(F32)
+        def do_transpose(h):
+            for x in range(HP // 2):
+                t = ps_t.tile([128, 2, 2, 128], F32, name="tps")
+                for y in range(2):
+                    a = 2 * x + y
                     for u in range(2):
-                        nc.tensor.transpose(t[:, y, u, :], words[:, u : 256 : 2], ident[:])
-                qps[h] = t
+                        words = wide[h][:, u, 128 * a : 128 * a + 128, :].rearrange("p w e -> p (w e)").bitcast(F32)
+                        nc.tensor.transpose(t[:, y, u, :], words, ident[:])
+                tps[h, x] = t
+            t = ps_t.tile([128, 2, 2, 128], F32, name="tps")
+            for y in range(HP // 2):
+                words = qraw[h][:, y, :].bitcast(F32)
+                for u in range(2):
+                    nc.tensor.transpose(t[:, y, u, :], words[:, u : 256 : 2], ident[:])
+            tps[h, 2] = t
 
-            def do_evict(h):
-                t = work.tile([128, HP * 128 * 4], BF16, name="dgrp", align_bytes=64)
-                words = t[:].bitcast(F32)
-                for x in range(HP // 2):
+        def do_evict(h):
+            t = work.tile([128, HP * 128 * 4], BF16, name="dgrp", align_bytes=64)
+            words = t[:].bitcast(F32)
+            for x in range(HP // 2):
+                if not any(s_widens(h, 2 * x + y) for y in range(2)):
                     nc.scalar.copy(
                         out=words[:, 512 * x : 512 * x + 512].rearrange("p (t r u) -> p t r u", t=2, u=2),
-                        in_=dps[h, x][:].rearrange("p t u r -> p t r u"))
-                dgrp[h] = t
-                t2 = work.tile([128, HP * 64 * 4], BF16, name="qgrp", align_bytes=64)
-                nc.scalar.copy(
-                    out=t2[:].bitcast(F32).rearrange("p (t r u) -> p t r u", t=2, u=2),
-                    in_=qps[h][:].rearrange("p t u r -> p t r u"))
-                qgrp[h] = t2
+                        in_=tps[h, x][:].rearrange("p t u r -> p t r u"))
+                    continue
+                for y in range(2):
+                    a = 2 * x + y
+                    if s_widens(h, a):
+                        nc.scalar.activation(
+                            out=t[:, 512 * a : 512 * a + 512].rearrange("p (r u e) -> p r u e", u=2, e=2),
+                            in_=tps[h, x][:, y].rearrange("p u r -> p (u r)").bitcast(BF16).rearrange("p (u r e) -> p r u e", u=2, e=2),
+                            func=COPY, scale=scp[:, h * HP + a : h * HP + a + 1])
+                    else:
+                        nc.scalar.copy(
+                            out=words[:, 256 * a : 256 * a + 256].rearrange("p (r u) -> p r u", u=2),
+                            in_=tps[h, x][:, y].rearrange("p u r -> p r u"))
+            dgrp[h] = t
+            t2 = work.tile([128, HP * 64 * 4], BF16, name="qgrp", align_bytes=64)
+            nc.scalar.copy(
+                out=t2[:].bitcast(F32).rearrange("p (t r u) -> p t r u", t=2, u=2),
+                in_=tps[h, 2][:].rearrange("p t u r -> p t r u"))
+            qgrp[h] = t2
 
-            def do_quant(h):
-                c = work.tile([128, HP * 128], U32, name="dcode", align_bytes=64)
-                s = work.tile([128, HP * 128], U8, name="dscal", align_bytes=64)
-                nc.vector.quantize_mx(out=c[:].bitcast(F8X4), scales=s[:], in_=dgrp[h][:])
-                dcod[h] = (c, s)
-                c = work.tile([128, HP * 64], U32, name="qcode", align_bytes=64)
-                s = work.tile([128, HP * 64], U8, name="qscal", align_bytes=64)
-                nc.vector.quantize_mx(out=c[:].bitcast(F8X4), scales=s[:], in_=qgrp[h][:])
-                qcod[h] = (c, s)
+        def do_scale(h):
+            for a in range(HP):
+                if not s_widens(h, a):
+                    z = dgrp[h][:, 512 * a : 512 * a + 512]
+                    nc.vector.tensor_scalar(out=z, in0=z, scalar1=scp[:, h * HP + a : h * HP + a + 1], scalar2=None, op0=ALU.mult)
 
-            def do_mx(h):
-                if h % 2 == 0:
-                    t = ps_m.tile([128, 2 * HP, LQ], F32, name="mps")
-                    mps[h // 2] = t
-                t = mps[h // 2]
+        def do_quant(h):
+            c = work.tile([128, HP * 128], U32, name="dcode", align_bytes=64)
+            s = work.tile([128, HP * 128], U8, name="dscal", align_bytes=64)
+            nc.vector.quantize_mx(out=c[:].bitcast(F8X4), scales=s[:], in_=dgrp[h][:])
+            dcod[h] = (c, s)
+            c = work.tile([128, HP * 64], U32, name="qcode", align_bytes=64)
+            s = work.tile([128, HP * 64], U8, name="qscal", align_bytes=64)
+            nc.vector.quantize_mx(out=c[:].bitcast(F8X4), scales=s[:], in_=qgrp[h][:])
+            qcod[h] = (c, s)
+
+        def do_mx(h):
+            if h % 2 == 0:
+                return
+            t = ps_m.tile([128, 2 * HP, LQ], F32, name="mps")
+            mps[h] = t
+            for h2 in (h - 1, h):
                 for a in range(HP):
                     nc.tensor.matmul_mx(
-                        out=t[:, (h % 2) * HP + a, :],
-                        lhsT=dcod[h][0][:, 128 * a : 128 * a + 128].bitcast(F8X4),
-                        lhsT_scale=dcod[h][1][:, 128 * a : 128 * a + 128],
-                        rhs=qcod[h][0][:, 64 * a : 64 * a + 64].bitcast(F8X4),
-                        rhs_scale=qcod[h][1][:, 64 * a : 64 * a + 64],
+                        out=t[:, (h2 % 2) * HP + a, :],
+                        lhsT=dcod[h2][0][:, 128 * a : 128 * a + 128].bitcast(F8X4),
+                        lhsT_scale=dcod[h2][1][:, 128 * a : 128 * a + 128],
+                        rhs=qcod[h2][0][:, 64 * a : 64 * a + 64].bitcast(F8X4),
+                        rhs_scale=qcod[h2][1][:, 64 * a : 64 * a + 64],
                         start=True, stop=True)
 
-            def do_mevict(h):
-                if h % 2 == 1:
-                    n0 = (h - 1) * HP
-                    nc.scalar.copy(
-                        out=m[:, 1 : LQ + 1, n0 : n0 + 2 * HP],
-                        in_=mps[h // 2][:].rearrange("p a i -> p i a"))
-
-            AHEAD = 4
-            with tc.manual_schedule():
-                for h in range(AHEAD):
-                    do_load(h)
-                nc.sync.dma_start(out=kern_b[:], in_=kern.rearrange("a b -> (a b)").partition_broadcast(128))
-                for it in range(-1, STEPS + 4):
-                    if 0 <= it + AHEAD + 1 < STEPS and it + AHEAD + 1 >= AHEAD:
-                        do_load(it + AHEAD + 1)
-                    if it + 1 < STEPS:
-                        do_widen(it + 1)
-                    if 0 <= it < STEPS:
-                        do_transpose(it)
-                        do_evict(it)
-                    if 0 <= it - 1 < STEPS:
-                        do_quant(it - 1)
-                    if 0 <= it - 2 < STEPS:
-                        do_mx(it - 2)
-                    if 0 <= it - 3 < STEPS:
-                        do_mevict(it - 3)
-                    if it == 2:
-                        nc.vector.tensor_scalar(out=mask[:, 0:1], in0=ident[:, 127:128], scalar1=-1.0, scalar2=1.0, op0=ALU.mult, op1=ALU.add)
-                        nc.vector.tensor_scalar(out=mask[:, 1:2], in0=ident[:, 0:1], scalar1=-1.0, scalar2=1.0, op0=ALU.mult, op1=ALU.add)
-                        nc.vector.tensor_scalar(out=kcol[:], in0=kern_b[:], scalar1=1.0 / math.sqrt(D), scalar2=None, op0=ALU.mult)
-                        kc = kcol[:].rearrange("p (u v) -> p u v", v=3)
-                        for v in (0, 2):
-                            mk = mask[:, v // 2 : v // 2 + 1]
-                            nc.vector.tensor_scalar(out=kc[:, :, v], in0=kc[:, :, v], scalar1=mk, scalar2=None, op0=ALU.mult)
-                        nc.vector.tensor_copy(out=perm_l[:, 1:128], in_=ident[:, 0:127])
-                        nc.vector.tensor_copy(out=perm_l[:, 0:1], in_=ident[:, 127:128])
-                        nc.vector.tensor_copy(out=perm_r[:, 0:127], in_=ident[:, 1:128])
-                        nc.vector.tensor_copy(out=perm_r[:, 127:128], in_=ident[:, 0:1])
-                for gg in range(4):
-                    nc.sync.dma_start(out=w_sb[:, gg, :].bitcast(I32), in_=w_words[gg].rearrange("p n t -> p (n t)").bitcast(I32))
-                nc.sync.dma_start(out=g_b[:], in_=g.partition_broadcast(128))
-                nc.sync.dma_start(out=b_b[:], in_=b.partition_broadcast(128))
-                for gg in range(4):
-                    for qd in range(4):
-                        nc.sync.dma_start(
-                            out=ws[32 * qd + 4 * gg : 32 * qd + 4 * gg + 4, :].bitcast(I32),
-                            in_=w_scales[gg, 4 * qd : 4 * qd + 4, :].bitcast(I32))
-
-        prod = ctx.enter_context(tc.tile_pool(name="prod", bufs=3))
-        hid = ctx.enter_context(tc.tile_pool(name="hid", bufs=2))
-        ps_c = ctx.enter_context(tc.psum_pool(name="ps_c", bufs=4))
-        ps_h = ctx.enter_context(tc.psum_pool(name="ps_h", bufs=1))
-        ps_y = ctx.enter_context(tc.psum_pool(name="ps_y", bufs=1))
-        y = [ps_y.tile([128, 512], F32, name="y%d" % x) for x in range(2)]
-        hh = big.tile([128, FEATS], BF16, name="hh", align_bytes=64)
-        perms = (perm_l, ident, perm_r)
-        prods = {}
-        cps = {}
+        def do_mevict(h):
+            if h % 2 == 0:
+                return
+            gi = h // SPG
+            if gi not in m:
+                t = grid.tile([128, RI + 2, B], F32, name="m")
+                nc.gpsimd.memset(t[:, 0, 0:GP], 0.0)
+                nc.gpsimd.memset(t[:, RI + 1, B - GP : B], 0.0)
+                m[gi] = t
+            n0 = (h - 1) % SPG * HP
+            nc.scalar.copy(
+                out=m[gi][:, 1 : RI + 1, :].rearrange("p i (x n) -> p i x n", x=NQ)[:, :, :, n0 : n0 + 2 * HP],
+                in_=mps[h][:].rearrange("p n (x i) -> p i x n", x=NQ))
+            if h % SPG == SPG - 1:
+                nc.gpsimd.tensor_copy(out=m[gi][:, 0, GP:B], in_=m[gi][:, RI, 0 : B - GP])
+                nc.gpsimd.tensor_copy(out=m[gi][:, RI + 1, 0 : B - GP], in_=m[gi][:, 1, GP:B])
 
         def rows(c, u):
-            return m[:, CH * c + u : CH * c + u + CH, :].rearrange("p i n -> p (i n)")
+            r0 = c % CPG * CH + u
+            return m[c // CPG][:, r0 : r0 + CH, :].rearrange("p i n -> p (i n)")
 
         def kc1(u, v):
             return kcol[:, 3 * u + v : 3 * u + v + 1]
 
-        SUMMED = (0, 2)
-        ON_V = [(2, 0), (2, 1), (2, 2)]
-
-        def do_prod(c):
-            t = {}
-            for u, v in ((1, 0), (1, 2), (1, 1), (0, 1)):
-                x = prod.tile([128, CH * B], F32, name="pr%d%d" % (u, v))
-                nc.scalar.activation(out=x[:], in_=rows(c, u), func=COPY, scale=kc1(u, v))
-                t[u, v] = x
-            for u, v in ON_V:
-                x = prod.tile([128, CH * B], F32, name="pr%d%d" % (u, v))
-                nc.vector.tensor_scalar(out=x[:], in0=rows(c, u), scalar1=kc1(u, v), scalar2=None, op0=ALU.mult)
-                t[u, v] = x
-            for v in SUMMED:
-                x = prod.tile([128, CH * B], F32, name="sum%d" % v)
-                nc.vector.scalar_tensor_tensor(out=x[:], in0=rows(c, 0), scalar=kc1(0, v), in1=t[1, v][:], op0=ALU.mult, op1=ALU.add)
-                t[1, v] = x
-            prods[c] = t
-
-        def do_conv(c):
-            ps = ps_c.tile([128, CH, LD], F32, name="cps")
+        def do_prod(c, part):
+            if part == 0:
+                prods[c] = {}
             t = prods[c]
-            keys = [(2, 0), (2, 1), (2, 2), (0, 1), (1, 1), (1, 0), (1, 2)]
-            for i in range(CH):
+            todo = (LAST if c >= CHUNKS - 6 else MAIN)[part]
+            for eng, u, v in todo:
+                lo = B * BAND if u == 1 else 0
+                if eng == "+":
+                    x = prod.tile([128, CH * B], F32, name="sum%d" % v)
+                    nc.vector.scalar_tensor_tensor(out=x[:], in0=rows(c, 0), scalar=kc1(0, v), in1=t[2, v][:], op0=ALU.mult, op1=ALU.add)
+                    t[2, v] = x
+                    continue
+                x = prod.tile([128, CH * B], F32, name="pr%d%d" % (u, v))
+                if eng == "S" or (eng == "A" and c % 2 == 0):
+                    nc.scalar.activation(out=x[:, lo:], in_=rows(c, u)[:, lo:], func=COPY, scale=kc1(u, v))
+                else:
+                    nc.vector.tensor_scalar(out=x[:, lo:], in0=rows(c, u)[:, lo:], scalar1=kc1(u, v), scalar2=None, op0=ALU.mult)
+                t[u, v] = x
+
+        def do_conv(c, part):
+            if part == 0:
+                ps = ps_c.tile([128, CH, LD], F32, name="cps")
+                cps[c] = ps
+            ps = cps[c]
+            t = prods[c]
+            for i in (2 * part, 2 * part + 1):
+                keys = [(u, v) for u, v in sorted(t) if i >= BAND or u != 1]
+                if i < BAND:
+                    nc.tensor.matmul(ps[:, i, :], m[c // CPG][:, c % CPG * CH + i + 1, :], band[:], start=True, stop=False)
                 for n, (u, v) in enumerate(keys):
                     nc.tensor.matmul(ps[:, i, :], t[u, v][:, B * i : B * i + B], perms[v][:],
-                                     start=(n == 0), stop=(n == len(keys) - 1), is_transpose=True)
-            cps[c] = ps
+                                     start=(n == 0 and i >= BAND), stop=(n == len(keys) - 1), is_transpose=True)
+
+        def halves(c):
+            return ((0, 1), (1, 2)) if c == CHUNKS - 1 else ((0, 2),)
 
         def do_pool(c):
             r = hid.tile([128, CH // 2, LD // 2], F32, name="pooled")
-            nc.vector.tensor_reduce(out=r[:], in_=cps[c][:].rearrange("p (a i) (b j) -> p a b i j", i=2, j=2), axis=AX.XY, op=ALU.max)
-            n = CH // 2 * LD // 2
-            nc.vector.scalar_tensor_tensor(out=hh[:, n * c : n * c + n], in0=r[:].rearrange("p a b -> p (a b)"), scalar=0.0,
-                                           in1=g_b[:, n * c : n * c + n], op0=ALU.max, op1=ALU.mult)
+            for lo, hi in halves(c):
+                nc.vector.tensor_reduce(out=r[:, lo:hi, :], in_=cps[c][:, 2 * lo : 2 * hi, :].rearrange("p (a i) (b j) -> p a b i j", i=2, j=2), axis=AX.XY, op=ALU.max)
+            pooled[c] = r
 
-        def do_hidden(gg):
-            hw = hh[:].bitcast(F32)
+        def do_gate(c):
+            gi, cc = c // CPG, c % CPG
+            if cc == 0:
+                t = hid.tile([128, FEATS // NQ], BF16, name="hh", align_bytes=64)
+                hh[gi] = t
+            n = LD // 2
+            for lo, hi in halves(c):
+                f0, f1 = n * (CH // 2 * cc + lo), n * (CH // 2 * cc + hi)
+                nc.vector.scalar_tensor_tensor(out=hh[gi][:, f0:f1], in0=pooled[c][:, lo:hi, :].rearrange("p a b -> p (a b)"), scalar=0.0,
+                                               in1=g_b[:, f0:f1], op0=ALU.max, op1=ALU.mult)
+
+        def do_turn(gi):
+            hw = hh[gi][:].bitcast(F32)
             t = ps_h.tile([128, 2, 128], F32, name="hps")
             for u in range(2):
-                nc.tensor.transpose(t[:, u, :], hw[:, 256 * gg + u : 256 * gg + 256 : 2], ident[:])
-            hg = hid.tile([128, 512], BF16, name="hg", align_bytes=64)
-            nc.scalar.copy(out=hg[:].bitcast(F32).rearrange("p (r u) -> p r u", u=2), in_=t[:].rearrange("p u r -> p r u"))
-            c = hid.tile([128, 128], U32, name="hcode", align_bytes=64)
-            s = hid.tile([128, 128], U8, name="hscal", align_bytes=64)
-            nc.vector.quantize_mx(out=c[:].bitcast(F8X4), scales=s[:], in_=hg[:])
-            for x in range(2):
-                nc.tensor.matmul_mx(
-                    out=y[x][:], lhsT=c[:].bitcast(F8X4), lhsT_scale=s[:],
-                    rhs=w_sb[:, gg, 512 * x : 512 * x + 512].bitcast(F8X4), rhs_scale=ws[4 * gg : 128, 512 * x : 512 * x + 512],
-                    start=(gg == 0), stop=(gg == 3))
+                nc.tensor.transpose(t[:, u, :], hw[:, u : 256 : 2], ident[:])
+            dst = hg[:].bitcast(F32).rearrange("p (x n u) -> p x n u", x=NQ, u=2)[:, :, GP * gi : GP * gi + GP, :]
+            src = t[:].rearrange("p u (x n) -> p x n u", x=NQ)
+            nc.scalar.copy(out=dst, in_=src)
 
-        per = CHUNKS // 4
+        def do_setup():
+            nc.vector.tensor_scalar(out=mask[:, 0:1], in0=ident[:, 127:128], scalar1=-1.0, scalar2=1.0, op0=ALU.mult, op1=ALU.add)
+            nc.vector.tensor_scalar(out=mask[:, 1:2], in0=ident[:, 0:1], scalar1=-1.0, scalar2=1.0, op0=ALU.mult, op1=ALU.add)
+            nc.vector.tensor_scalar(out=kcol[:], in0=kern_b[:], scalar1=1.0 / math.sqrt(D), scalar2=None, op0=ALU.mult)
+            kc = kcol[:].rearrange("p (u v) -> p u v", v=3)
+            for v in (0, 2):
+                mk = mask[:, v // 2 : v // 2 + 1]
+                nc.vector.tensor_scalar(out=kc[:, :, v], in0=kc[:, :, v], scalar1=mk, scalar2=None, op0=ALU.mult)
+            nc.vector.tensor_copy(out=perm_l[:, 1:128], in_=ident[:, 0:127])
+            nc.vector.tensor_copy(out=perm_l[:, 0:1], in_=ident[:, 127:128])
+            nc.vector.tensor_copy(out=perm_r[:, 0:127], in_=ident[:, 1:128])
+            nc.vector.tensor_copy(out=perm_r[:, 127:128], in_=ident[:, 0:1])
+            nc.vector.tensor_scalar(out=band[:], in0=ident[:], scalar1=kcol[:, 4:5], scalar2=None, op0=ALU.mult)
+            nc.vector.scalar_tensor_tensor(out=band[:], in0=perm_l[:], scalar=kcol[:, 3:4], in1=band[:], op0=ALU.mult, op1=ALU.add)
+            nc.vector.scalar_tensor_tensor(out=band[:], in0=perm_r[:], scalar=kcol[:, 5:6], in1=band[:], op0=ALU.mult, op1=ALU.add)
+
+        def do_late_loads():
+            for gg in range(4):
+                nc.sync.dma_start(out=w_sb[:, gg, :].bitcast(I32), in_=w_words[gg].rearrange("p n t -> p (n t)").bitcast(I32))
+            nc.sync.dma_start(out=b_b[:], in_=b.partition_broadcast(128))
+            for gg in range(4):
+                for qd in range(4):
+                    nc.sync.dma_start(
+                        out=ws[32 * qd + 4 * gg : 32 * qd + 4 * gg + 4, :].bitcast(I32),
+                        in_=w_scales[gg, 4 * qd : 4 * qd + 4, :].bitcast(I32))
+
+        def prod_step(c):
+            return SPG * (c // CPG + 1) + 5 + 2 * (c % CPG)
+
+        plan = {}
+        for c in range(CHUNKS):
+            t0 = prod_step(c)
+            for dt, what in ((0, ("prod", c, 0)), (1, ("prod", c, 1)), (2, ("conv", c, 0)), (3, ("conv", c, 1)), (4, ("pool", c)), (4, ("gate", c))):
+                plan.setdefault(t0 + dt, []).append(what)
+            if c % CPG == CPG - 1:
+                plan.setdefault(t0 + 5, []).append(("turn", c // CPG))
+
         with tc.manual_schedule():
-            for it in range(CHUNKS + 3):
-                if it < CHUNKS:
-                    do_prod(it)
-                if 0 <= it - 1 < CHUNKS:
-                    do_conv(it - 1)
-                if 0 <= it - 2 < CHUNKS:
-                    do_pool(it - 2)
-                    if (it - 2) % per == per - 1:
-                        do_hidden((it - 2) // per)
+            for h in range(AHEAD):
+                do_load(h)
+            nc.sync.dma_start(out=kern_b[:], in_=kern.rearrange("a b -> (a b)").partition_broadcast(128))
+            for x in range(NQ):
+                nc.sync.dma_start(out=g_b[32 * x : 32 * x + 32, :], in_=g.rearrange("(x f) -> x f", x=NQ)[x].partition_broadcast(32))
+            do_widen(0, False)
+            do_widen(0, True)
+            for it in range(max(plan) + 1):
+                todo = plan.get(it, [])
+                if it + AHEAD < STEPS:
+                    do_load(it + AHEAD)
+                if it + AHEAD == STEPS:
+                    do_late_loads()
+                if it < STEPS:
+                    do_transpose(it)
+                if 0 <= it - 1 < STEPS:
+                    do_scale(it - 1)
+                for w in todo:
+                    if w[0] == "pool":
+                        do_pool(w[1])
+                for w in todo:
+                    if w[0] == "conv":
+                        do_conv(w[1], w[2])
+                if it + 1 < STEPS:
+                    do_widen(it + 1, False)
+                for w in todo:
+                    if w[0] == "prod":
+                        do_prod(w[1], w[2])
+                if 0 <= it - 1 < STEPS:
+                    do_quant(it - 1)
+                for w in todo:
+                    if w[0] == "gate":
+                        do_gate(w[1])
+                    if w[0] == "turn":
+                        do_turn(w[1])
+                if 0 <= it - 2 < STEPS:
+                    do_mx(it - 2)
+                if it < STEPS:
+                    do_evict(it)
+                if it + 1 < STEPS:
+                    do_widen(it + 1, True)
+                if 0 <= it - 2 < STEPS:
+                    do_mevict(it - 2)
+                if it == 2:
+                    do_setup()
+            y = []
+            for x in range(2):
+                t = ps_t.tile([128, 512], F32, name="tps")
+                y.append(t)
+            hc = []
+            for gg in range(4):
+                c = hid.tile([128, 128], U32, name="hcode%d" % gg, align_bytes=64)
+                s = hid.tile([128, 128], U8, name="hscal%d" % gg, align_bytes=64)
+                nc.vector.quantize_mx(out=c[:].bitcast(F8X4), scales=s[:], in_=hg[:, 512 * gg : 512 * gg + 512])
+                hc.append((c, s))
+            for x in range(2):
+                for gg in range(4):
+                    c, s = hc[gg]
+                    nc.tensor.matmul_mx(
+                        out=y[x][:], lhsT=c[:].bitcast(F8X4), lhsT_scale=s[:],
+                        rhs=w_sb[:, gg, 512 * x : 512 * x + 512].bitcast(F8X4), rhs_scale=ws[4 * gg : 128, 512 * x : 512 * x + 512],
+                        start=(gg == 0), stop=(gg == 3))
             for x in range(2):
                 t = hid.tile([128, 512], F32, name="ysum")
-                nc.vector.tensor_tensor(out=t[:], in0=y[x][:], in1=b_b[:, 512 * x : 512 * x + 512], op=ALU.add)
                 o = hid.tile([128, 512], F32, name="yout")
-                nc.scalar.activation(out=o[:], in_=t[:], func=mybir.ActivationFunctionType.Relu)
+                for z0 in range(0, 512, 256):
+                    z = slice(z0, z0 + 256)
+                    nc.vector.tensor_tensor(out=t[:, z], in0=y[x][:, z], in1=b_b[:, 512 * x + z0 : 512 * x + z0 + 256], op=ALU.add)
+                    nc.scalar.activation(out=o[:, z], in_=t[:, z], func=RELU)
                 nc.sync.dma_start(out=out[:, 512 * x : 512 * x + 512], in_=o[:])

@@ -31,7 +31,7 @@ CPG = RI // CH
 CHUNKS = NQ * CPG
 AHEAD = 5
 BAND = 2
-MAIN = ((("S", 2, 0), ("S", 2, 1), ("V", 0, 1), ("V", 1, 0)), (("S", 2, 2), ("A", 0, 2), ("+", 0, 0), ("V", 1, 1), ("V", 1, 2)))
+MAIN = ((("S", 2, 0), ("S", 2, 2), ("V", 1, 0), ("V", 1, 1)), (("S", 2, 1), ("A", 0, 1), ("V", 1, 2), ("+", 0, 0), ("+", 0, 2)))
 LAST = ((("S", 2, 0), ("S", 2, 2), ("V", 1, 0), ("V", 1, 1)), (("S", 2, 1), ("A", 0, 1), ("V", 1, 2), ("+", 0, 0), ("+", 0, 2)))
 
 
@@ -93,12 +93,9 @@ def tile_matchpyramiddotgridmlphidden_d2p_kernel(tc, q, d_bytes, d_scale, kern, 
         def do_widen(h, on_s):
             if on_s:
                 return
-            t = work.tile([128, 2, HP * 128, 2], BF16, name="wide", align_bytes=64)
+            t = work.tile([128, HP, D], BF16, name="wide", align_bytes=64)
             for a, n in parts(h):
-                nc.vector.tensor_scalar(
-                    out=t[:, :, 128 * a : 128 * (a + n), :].rearrange("p u w e -> p w u e"),
-                    in0=dby[h][:, a : a + n, :].rearrange("p a k -> p (a k)").bitcast(F8).rearrange("p (w u e) -> p w u e", u=2, e=2),
-                    scalar1=ones[:], scalar2=None, op0=ALU.mult)
+                nc.vector.tensor_copy(out=t[:, a : a + n, :].rearrange("p a k -> p (a k)"), in_=dby[h][:, a : a + n, :].rearrange("p a k -> p (a k)").bitcast(F8))
             wide[h] = t
 
         def do_transpose(h):
@@ -107,8 +104,8 @@ def tile_matchpyramiddotgridmlphidden_d2p_kernel(tc, q, d_bytes, d_scale, kern, 
                 for y in range(2):
                     a = 2 * x + y
                     for u in range(2):
-                        words = wide[h][:, u, 128 * a : 128 * a + 128, :].rearrange("p w e -> p (w e)").bitcast(F32)
-                        nc.tensor.transpose(t[:, y, u, :], words, ident[:])
+                        words = wide[h][:, a, :].bitcast(F32)
+                        nc.tensor.transpose(t[:, y, u, :], words[:, u : 256 : 2], ident[:])
                 tps[h, x] = t
             t = ps_t.tile([128, 2, 2, 128], F32, name="tps")
             for y in range(HP // 2):
@@ -203,7 +200,7 @@ def tile_matchpyramiddotgridmlphidden_d2p_kernel(tc, q, d_bytes, d_scale, kern, 
             if part == 0:
                 prods[c] = {}
             t = prods[c]
-            todo = (LAST if c >= CHUNKS - 6 else MAIN)[part]
+            todo = (LAST if c >= CHUNKS - 4 else MAIN)[part]
             for eng, u, v in todo:
                 lo = B * BAND if u == 1 else 0
                 if eng == "+":

from contextlib import ExitStack
import math

import concourse.mybir as mybir
from concourse.masks import make_identity

F32 = mybir.dt.float32
BF16 = mybir.dt.bfloat16
U32 = mybir.dt.uint32
U8 = mybir.dt.uint8
I32 = mybir.dt.int32
F8 = mybir.dt.float8_e4m3fn
F8X4 = mybir.dt.float8_e4m3fn_x4
ALU = mybir.AluOpType
COPY = mybir.ActivationFunctionType.Copy
RELU = mybir.ActivationFunctionType.Relu
AX = mybir.AxisListType

B, LQ, LD, D, H = 128, 64, 128, 512, 1024
FEATS = 2048
FLOPS = 2 * B * LQ * LD * D + 2 * B * FEATS * H + 18 * B * LQ * LD

HP = 4
STEPS = B // HP
NQ = 4
GP = B // NQ
SPG = STEPS // NQ
RI = LQ // NQ
CH = 4
CPG = RI // CH
CHUNKS = NQ * CPG
AHEAD = 5
BAND = 2
MAIN = ((("S", 2, 0), ("S", 2, 2), ("V", 1, 0), ("V", 1, 1)), (("S", 2, 1), ("A", 0, 1), ("V", 1, 2), ("+", 0, 0), ("+", 0, 2)))
LAST = ((("S", 2, 0), ("S", 2, 2), ("V", 1, 0), ("V", 1, 1)), (("S", 2, 1), ("A", 0, 1), ("V", 1, 2), ("+", 0, 0), ("+", 0, 2)))


def tile_matchpyramiddotgridmlphidden_d2p_kernel(tc, q, d_bytes, d_scale, kern, g, w_words, w_scales, b, out):
    nc = tc.nc
    with ExitStack() as ctx:
        const = ctx.enter_context(tc.tile_pool(name="const", bufs=1))
        load = ctx.enter_context(tc.tile_pool(name="load", bufs=6))
        work = ctx.enter_context(tc.tile_pool(name="work", bufs=3))
        grid = ctx.enter_context(tc.tile_pool(name="grid", bufs=3))
        prod = ctx.enter_context(tc.tile_pool(name="prod", bufs=2))
        hid = ctx.enter_context(tc.tile_pool(name="hid", bufs=2))
        ps_t = ctx.enter_context(tc.psum_pool(name="ps_t", bufs=4))
        ps_m = ctx.enter_context(tc.psum_pool(name="ps_m", bufs=1))
        ps_c = ctx.enter_context(tc.psum_pool(name="ps_c", bufs=2))
        ps_h = ctx.enter_context(tc.psum_pool(name="ps_h", bufs=1))

        ident = const.tile([128, 128], F32, name="ident")
        make_identity(nc, ident[:])
        scl = const.tile([128, B * 4], F32, name="scl")
        nc.scalar.dma_start(out=scl[:], in_=d_scale.rearrange("a o q -> (a o q)").partition_broadcast(128))
        ones = const.tile([128, 1], F32, name="ones")
        nc.vector.memset(ones[:], 1.0)
        scp = const.tile([128, B], F32, name="scp")
        for x in range(4):
            nc.gpsimd.tensor_copy(out=scp[32 * x : 32 * x + 32, :], in_=scl[32 * x : 32 * x + 32, :].rearrange("p (n x) -> p n x", x=4)[:, :, x])
        kern_b = const.tile([128, 9], BF16, name="kern_b")
        perm_l = const.tile([128, 128], F32, name="perm_l")
        perm_r = const.tile([128, 128], F32, name="perm_r")
        kcol = const.tile([128, 9], F32, name="kcol")
        band = const.tile([128, 128], F32, name="band")
        mask = const.tile([128, 2], F32, name="mask")
        g_b = const.tile([128, FEATS // NQ], BF16, name="g_b")
        b_b = const.tile([128, H], BF16, name="b_b")
        w_sb = const.tile([128, 4, H], U32, name="w_sb", align_bytes=64)
        ws = const.tile([128, H], U8, name="ws", align_bytes=64)
        hg = const.tile([128, 4 * B * 4], BF16, name="hg", align_bytes=64)
        nc.gpsimd.memset(ws[:].bitcast(I32), 0)

        dby, qraw, wide, dgrp, qgrp, dcod, qcod, tps, mps, m, prods, cps, pooled, hh = ({} for n in range(14))
        perms = (perm_l, ident, perm_r)

        def s_widens(h, a):
            return a >= 2

        def parts(h):
            return [(a, 1) for a in range(HP)] if h == 0 else [(0, HP)]

        def do_load(h):
            n0 = h * HP
            t = load.tile([128, HP, D], U8, name="dby", align_bytes=64)
            for a, n in parts(h):
                nc.sync.dma_start(out=t[:, a : a + n, :], in_=d_bytes[n0 + a : n0 + a + n].rearrange("a r k -> r a k"))
            dby[h] = t
            t2 = load.tile([128, HP // 2, D], BF16, name="qraw", align_bytes=64)
            nc.sync.dma_start(out=t2[:], in_=q[n0 : n0 + HP].rearrange("(t a) i k -> (a i) t k", a=2))
            qraw[h] = t2

        def do_widen(h, on_s):
            if on_s:
                return
            t = work.tile([128, HP, D], BF16, name="wide", align_bytes=64)
            for a, n in parts(h):
                nc.vector.tensor_copy(out=t[:, a : a + n, :].rearrange("p a k -> p (a k)"), in_=dby[h][:, a : a + n, :].rearrange("p a k -> p (a k)").bitcast(F8))
            wide[h] = t

        def do_transpose(h):
            for x in range(HP // 2):
                t = ps_t.tile([128, 2, 2, 128], F32, name="tps")
                for y in range(2):
                    a = 2 * x + y
                    for u in range(2):
                        words = wide[h][:, a, :].bitcast(F32)
                        nc.tensor.transpose(t[:, y, u, :], words[:, u : 256 : 2], ident[:])
                tps[h, x] = t
            t = ps_t.tile([128, 2, 2, 128], F32, name="tps")
            for y in range(HP // 2):
                words = qraw[h][:, y, :].bitcast(F32)
                for u in range(2):
                    nc.tensor.transpose(t[:, y, u, :], words[:, u : 256 : 2], ident[:])
            tps[h, 2] = t

        def do_evict(h):
            t = work.tile([128, HP * 128 * 4], BF16, name="dgrp", align_bytes=64)
            words = t[:].bitcast(F32)
            for x in range(HP // 2):
                if not any(s_widens(h, 2 * x + y) for y in range(2)):
                    nc.scalar.copy(
                        out=words[:, 512 * x : 512 * x + 512].rearrange("p (t r u) -> p t r u", t=2, u=2),
                        in_=tps[h, x][:].rearrange("p t u r -> p t r u"))
                    continue
                for y in range(2):
                    a = 2 * x + y
                    if s_widens(h, a):
                        nc.scalar.activation(
                            out=t[:, 512 * a : 512 * a + 512].rearrange("p (r u e) -> p r u e", u=2, e=2),
                            in_=tps[h, x][:, y].rearrange("p u r -> p (u r)").bitcast(BF16).rearrange("p (u r e) -> p r u e", u=2, e=2),
                            func=COPY, scale=scp[:, h * HP + a : h * HP + a + 1])
                    else:
                        nc.scalar.copy(
                            out=words[:, 256 * a : 256 * a + 256].rearrange("p (r u) -> p r u", u=2),
                            in_=tps[h, x][:, y].rearrange("p u r -> p r u"))
            dgrp[h] = t
            t2 = work.tile([128, HP * 64 * 4], BF16, name="qgrp", align_bytes=64)
            nc.scalar.copy(
                out=t2[:].bitcast(F32).rearrange("p (t r u) -> p t r u", t=2, u=2),
                in_=tps[h, 2][:].rearrange("p t u r -> p t r u"))
            qgrp[h] = t2

        def do_scale(h):
            for a in range(HP):
                if not s_widens(h, a):
                    z = dgrp[h][:, 512 * a : 512 * a + 512]
                    nc.vector.tensor_scalar(out=z, in0=z, scalar1=scp[:, h * HP + a : h * HP + a + 1], scalar2=None, op0=ALU.mult)

        def do_quant(h):
            c = work.tile([128, HP * 128], U32, name="dcode", align_bytes=64)
            s = work.tile([128, HP * 128], U8, name="dscal", align_bytes=64)
            nc.vector.quantize_mx(out=c[:].bitcast(F8X4), scales=s[:], in_=dgrp[h][:])
            dcod[h] = (c, s)
            c = work.tile([128, HP * 64], U32, name="qcode", align_bytes=64)
            s = work.tile([128, HP * 64], U8, name="qscal", align_bytes=64)
            nc.vector.quantize_mx(out=c[:].bitcast(F8X4), scales=s[:], in_=qgrp[h][:])
            qcod[h] = (c, s)

        def do_mx(h):
            if h % 2 == 0:
                return
            t = ps_m.tile([128, 2 * HP, LQ], F32, name="mps")
            mps[h] = t
            for h2 in (h - 1, h):
                for a in range(HP):
                    nc.tensor.matmul_mx(
                        out=t[:, (h2 % 2) * HP + a, :],
                        lhsT=dcod[h2][0][:, 128 * a : 128 * a + 128].bitcast(F8X4),
                        lhsT_scale=dcod[h2][1][:, 128 * a : 128 * a + 128],
                        rhs=qcod[h2][0][:, 64 * a : 64 * a + 64].bitcast(F8X4),
                        rhs_scale=qcod[h2][1][:, 64 * a : 64 * a + 64],
                        start=True, stop=True)

        def do_mevict(h):
            if h % 2 == 0:
                return
            gi = h // SPG
            if gi not in m:
                t = grid.tile([128, RI + 2, B], F32, name="m")
                nc.gpsimd.memset(t[:, 0, 0:GP], 0.0)
                nc.gpsimd.memset(t[:, RI + 1, B - GP : B], 0.0)
                m[gi] = t
            n0 = (h - 1) % SPG * HP
            nc.scalar.copy(
                out=m[gi][:, 1 : RI + 1, :].rearrange("p i (x n) -> p i x n", x=NQ)[:, :, :, n0 : n0 + 2 * HP],
                in_=mps[h][:].rearrange("p n (x i) -> p i x n", x=NQ))
            if h % SPG == SPG - 1:
                nc.gpsimd.tensor_copy(out=m[gi][:, 0, GP:B], in_=m[gi][:, RI, 0 : B - GP])
                nc.gpsimd.tensor_copy(out=m[gi][:, RI + 1, 0 : B - GP], in_=m[gi][:, 1, GP:B])

        def rows(c, u):
            r0 = c % CPG * CH + u
            return m[c // CPG][:, r0 : r0 + CH, :].rearrange("p i n -> p (i n)")

        def kc1(u, v):
            return kcol[:, 3 * u + v : 3 * u + v + 1]

        def do_prod(c, part):
            if part == 0:
                prods[c] = {}
            t = prods[c]
            todo = (LAST if c >= CHUNKS - 4 else MAIN)[part]
            for eng, u, v in todo:
                lo = B * BAND if u == 1 else 0
                if eng == "+":
                    x = prod.tile([128, CH * B], F32, name="sum%d" % v)
                    nc.vector.scalar_tensor_tensor(out=x[:], in0=rows(c, 0), scalar=kc1(0, v), in1=t[2, v][:], op0=ALU.mult, op1=ALU.add)
                    t[2, v] = x
                    continue
                x = prod.tile([128, CH * B], F32, name="pr%d%d" % (u, v))
                if eng == "S" or (eng == "A" and c % 2 == 0):
                    nc.scalar.activation(out=x[:, lo:], in_=rows(c, u)[:, lo:], func=COPY, scale=kc1(u, v))
                else:
                    nc.vector.tensor_scalar(out=x[:, lo:], in0=rows(c, u)[:, lo:], scalar1=kc1(u, v), scalar2=None, op0=ALU.mult)
                t[u, v] = x

        def do_conv(c, part):
            if part == 0:
                ps = ps_c.tile([128, CH, LD], F32, name="cps")
                cps[c] = ps
            ps = cps[c]
            t = prods[c]
            for i in (2 * part, 2 * part + 1):
                keys = [(u, v) for u, v in sorted(t) if i >= BAND or u != 1]
                if i < BAND:
                    nc.tensor.matmul(ps[:, i, :], m[c // CPG][:, c % CPG * CH + i + 1, :], band[:], start=True, stop=False)
                for n, (u, v) in enumerate(keys):
                    nc.tensor.matmul(ps[:, i, :], t[u, v][:, B * i : B * i + B], perms[v][:],
                                     start=(n == 0 and i >= BAND), stop=(n == len(keys) - 1), is_transpose=True)

        def halves(c):
            return ((0, 1), (1, 2)) if c == CHUNKS - 1 else ((0, 2),)

        def do_pool(c):
            r = hid.tile([128, CH // 2, LD // 2], F32, name="pooled")
            for lo, hi in halves(c):
                nc.vector.tensor_reduce(out=r[:, lo:hi, :], in_=cps[c][:, 2 * lo : 2 * hi, :].rearrange("p (a i) (b j) -> p a b i j", i=2, j=2), axis=AX.XY, op=ALU.max)
            pooled[c] = r

        def do_gate(c):
            gi, cc = c // CPG, c % CPG
            if cc == 0:
                t = hid.tile([128, FEATS // NQ], BF16, name="hh", align_bytes=64)
                hh[gi] = t
            n = LD // 2
            for lo, hi in halves(c):
                f0, f1 = n * (CH // 2 * cc + lo), n * (CH // 2 * cc + hi)
                nc.vector.scalar_tensor_tensor(out=hh[gi][:, f0:f1], in0=pooled[c][:, lo:hi, :].rearrange("p a b -> p (a b)"), scalar=0.0,
                                               in1=g_b[:, f0:f1], op0=ALU.max, op1=ALU.mult)

        def do_turn(gi):
            hw = hh[gi][:].bitcast(F32)
            t = ps_h.tile([128, 2, 128], F32, name="hps")
            for u in range(2):
                nc.tensor.transpose(t[:, u, :], hw[:, u : 256 : 2], ident[:])
            dst = hg[:].bitcast(F32).rearrange("p (x n u) -> p x n u", x=NQ, u=2)[:, :, GP * gi : GP * gi + GP, :]
            src = t[:].rearrange("p u (x n) -> p x n u", x=NQ)
            nc.scalar.copy(out=dst, in_=src)

        def do_setup():
            nc.vector.tensor_scalar(out=mask[:, 0:1], in0=ident[:, 127:128], scalar1=-1.0, scalar2=1.0, op0=ALU.mult, op1=ALU.add)
            nc.vector.tensor_scalar(out=mask[:, 1:2], in0=ident[:, 0:1], scalar1=-1.0, scalar2=1.0, op0=ALU.mult, op1=ALU.add)
            nc.vector.tensor_scalar(out=kcol[:], in0=kern_b[:], scalar1=1.0 / math.sqrt(D), scalar2=None, op0=ALU.mult)
            kc = kcol[:].rearrange("p (u v) -> p u v", v=3)
            for v in (0, 2):
                mk = mask[:, v // 2 : v // 2 + 1]
                nc.vector.tensor_scalar(out=kc[:, :, v], in0=kc[:, :, v], scalar1=mk, scalar2=None, op0=ALU.mult)
            nc.vector.tensor_copy(out=perm_l[:, 1:128], in_=ident[:, 0:127])
            nc.vector.tensor_copy(out=perm_l[:, 0:1], in_=ident[:, 127:128])
            nc.vector.tensor_copy(out=perm_r[:, 0:127], in_=ident[:, 1:128])
            nc.vector.tensor_copy(out=perm_r[:, 127:128], in_=ident[:, 0:1])
            nc.vector.tensor_scalar(out=band[:], in0=ident[:], scalar1=kcol[:, 4:5], scalar2=None, op0=ALU.mult)
            nc.vector.scalar_tensor_tensor(out=band[:], in0=perm_l[:], scalar=kcol[:, 3:4], in1=band[:], op0=ALU.mult, op1=ALU.add)
            nc.vector.scalar_tensor_tensor(out=band[:], in0=perm_r[:], scalar=kcol[:, 5:6], in1=band[:], op0=ALU.mult, op1=ALU.add)

        def do_late_loads():
            for gg in range(4):
                nc.sync.dma_start(out=w_sb[:, gg, :].bitcast(I32), in_=w_words[gg].rearrange("p n t -> p (n t)").bitcast(I32))
            nc.sync.dma_start(out=b_b[:], in_=b.partition_broadcast(128))
            for gg in range(4):
                for qd in range(4):
                    nc.sync.dma_start(
                        out=ws[32 * qd + 4 * gg : 32 * qd + 4 * gg + 4, :].bitcast(I32),
                        in_=w_scales[gg, 4 * qd : 4 * qd + 4, :].bitcast(I32))

        def prod_step(c):
            return SPG * (c // CPG + 1) + 5 + 2 * (c % CPG)

        plan = {}
        for c in range(CHUNKS):
            t0 = prod_step(c)
            for dt, what in ((0, ("prod", c, 0)), (1, ("prod", c, 1)), (2, ("conv", c, 0)), (3, ("conv", c, 1)), (4, ("pool", c)), (4, ("gate", c))):
                plan.setdefault(t0 + dt, []).append(what)
            if c % CPG == CPG - 1:
                plan.setdefault(t0 + 5, []).append(("turn", c // CPG))

        with tc.manual_schedule():
            for h in range(AHEAD):
                do_load(h)
            nc.sync.dma_start(out=kern_b[:], in_=kern.rearrange("a b -> (a b)").partition_broadcast(128))
            for x in range(NQ):
                nc.sync.dma_start(out=g_b[32 * x : 32 * x + 32, :], in_=g.rearrange("(x f) -> x f", x=NQ)[x].partition_broadcast(32))
            do_widen(0, False)
            do_widen(0, True)
            for it in range(max(plan) + 1):
                todo = plan.get(it, [])
                if it + AHEAD < STEPS:
                    do_load(it + AHEAD)
                if it + AHEAD == STEPS:
                    do_late_loads()
                if it < STEPS:
                    do_transpose(it)
                if 0 <= it - 1 < STEPS:
                    do_scale(it - 1)
                for w in todo:
                    if w[0] == "pool":
                        do_pool(w[1])
                for w in todo:
                    if w[0] == "conv":
                        do_conv(w[1], w[2])
                if it + 1 < STEPS:
                    do_widen(it + 1, False)
                for w in todo:
                    if w[0] == "prod":
                        do_prod(w[1], w[2])
                if 0 <= it - 1 < STEPS:
                    do_quant(it - 1)
                for w in todo:
                    if w[0] == "gate":
                        do_gate(w[1])
                    if w[0] == "turn":
                        do_turn(w[1])
                if 0 <= it - 2 < STEPS:
                    do_mx(it - 2)
                if it < STEPS:
                    do_evict(it)
                if it + 1 < STEPS:
                    do_widen(it + 1, True)
                if 0 <= it - 2 < STEPS:
                    do_mevict(it - 2)
                if it == 2:
                    do_setup()
            y = []
            for x in range(2):
                t = ps_t.tile([128, 512], F32, name="tps")
                y.append(t)
            hc = []
            for gg in range(4):
                c = hid.tile([128, 128], U32, name="hcode%d" % gg, align_bytes=64)
                s = hid.tile([128, 128], U8, name="hscal%d" % gg, align_bytes=64)
                nc.vector.quantize_mx(out=c[:].bitcast(F8X4), scales=s[:], in_=hg[:, 512 * gg : 512 * gg + 512])
                hc.append((c, s))
            for x in range(2):
                for gg in range(4):
                    c, s = hc[gg]
                    nc.tensor.matmul_mx(
                        out=y[x][:], lhsT=c[:].bitcast(F8X4), lhsT_scale=s[:],
                        rhs=w_sb[:, gg, 512 * x : 512 * x + 512].bitcast(F8X4), rhs_scale=ws[4 * gg : 128, 512 * x : 512 * x + 512],
                        start=(gg == 0), stop=(gg == 3))
            for x in range(2):
                t = hid.tile([128, 512], F32, name="ysum")
                o = hid.tile([128, 512], F32, name="yout")
                for z0 in range(0, 512, 256):
                    z = slice(z0, z0 + 256)
                    nc.vector.tensor_tensor(out=t[:, z], in0=y[x][:, z], in1=b_b[:, 512 * x + z0 : 512 * x + z0 + 256], op=ALU.add)
                    nc.scalar.activation(out=o[:, z], in_=t[:, z], func=RELU)
                nc.sync.dma_start(out=out[:, 512 * x : 512 * x + 512], in_=o[:])
